import numpy as np
import ml_dtypes


def mxq(x, axis, fmt="e4m3"):
    dtype, down = {"e4m3": (ml_dtypes.float8_e4m3fn, 7), "e5m2": (ml_dtypes.float8_e5m2, 14)}[fmt]
    v = np.moveaxis(np.asarray(x, np.float32).astype(ml_dtypes.bfloat16).astype(np.float64), axis, -1)
    blocks = v.reshape(v.shape[:-1] + (-1, 32))
    amax = np.abs(blocks).max(-1, keepdims=True)
    byte = np.maximum(np.where(amax > 0, np.frexp(amax)[1] - 1 + 127, 0) - down, 1)
    scale = np.exp2(byte - 127.0)
    codes = (blocks / scale).astype(np.float32).astype(dtype).astype(np.float64)
    return np.moveaxis((codes * scale).reshape(v.shape), -1, axis)


WIDE = False


def mx_kscale(k):
    if not WIDE:
        return np.ones(k)
    levels = np.array([10, -10, 5, -5, 0])
    if k % 512:
        return np.exp2(np.random.permutation(np.resize(levels, k // 32))).repeat(32)
    a = np.empty((k // 512, 16))
    for p in range(k // 512):
        a[p, :8] = np.random.permutation(np.resize(levels, 8))
        for g in range(8):
            far = levels[np.abs(levels - a[p, g]) >= 10]
            a[p, g + 8] = far[np.random.randint(len(far))]
    return np.exp2(a.ravel()).repeat(32)


def f64(x):
    return np.asarray(x).astype(np.float64)


def striped(idx):
    return np.tile(idx.reshape(-1, 16).T, (8, 1)).astype(np.uint16)


def unstriped(offs):
    return offs[:16].T.reshape(-1).astype(np.int64)


E2M1 = np.array([0.0, 0.5, 1.0, 1.5, 2.0, 3.0, 4.0, 6.0, -0.0, -0.5, -1.0, -1.5, -2.0, -3.0, -4.0, -6.0])


def pack_weight(w, fmt):
    k, n = w.shape
    w = f64(np.asarray(w, np.float32).astype(ml_dtypes.bfloat16)).reshape(k // 32, 32, n)
    amax = np.abs(w).max(1)
    if fmt == "e4m3":
        byte = np.frexp(amax)[1] - 1 + 127 - 7
    else:
        mant, ex = np.frexp(amax / 6.0)
        byte = np.where(mant > 0.5, ex, ex - 1) + 127
    byte = np.clip(np.where(amax > 0, byte, 1), 1, 254)
    scaled = (w * np.exp2(127.0 - byte)[:, None, :]).reshape(k, n).astype(np.float32)
    by_word = np.ascontiguousarray(scaled.reshape(k // 512, 128, 4, n).transpose(0, 1, 3, 2))
    if fmt == "e4m3":
        words = by_word.astype(ml_dtypes.float8_e4m3fn).view(np.uint8)
    else:
        c = by_word.astype(ml_dtypes.float4_e2m1fn).view(np.uint8) & 0xF
        words = (c[..., 0::2] | (c[..., 1::2] << 4)).reshape(k // 512, 128, 2 * n)
    return np.ascontiguousarray(words), np.ascontiguousarray(byte.astype(np.uint8).reshape(k // 512, 16, n))


def unpack_weight(words, scales, fmt):
    g, _, n = scales.shape
    words = np.ascontiguousarray(words).reshape(g, 128, n, -1)
    if fmt == "e4m3":
        vals = words.view(ml_dtypes.float8_e4m3fn).astype(np.float64)
    else:
        nib = np.empty((g, 128, n, 4), np.uint8)
        nib[..., 0::2] = words & 0xF
        nib[..., 1::2] = words >> 4
        vals = E2M1[nib]
    vals = vals * np.repeat(np.exp2(scales.astype(np.float64) - 127.0), 8, axis=1)[..., None]
    return vals.transpose(0, 1, 3, 2).reshape(g * 512, n)


def gelu(v):
    return 0.5 * v * (1.0 + np.tanh(np.sqrt(2.0 / np.pi) * (v + 0.044715 * v**3)))


K, H, T, S, T2, P = 1024, 1024, 2048, 1024, 2048, 1024

def setup_inputs():
    n = np.random.standard_normal
    s = mx_kscale(K)[:, None]
    u = mx_kscale(H)[:, None]
    tab_words, tab_scales = pack_weight(n((K, T)) * s, "e4m3")
    w1 = (n((K, H)) / np.sqrt(K) / s * u.T).astype(np.float32)
    b1 = (0.5 * n(H) * u[:, 0]).astype(np.float32)
    base = (n((H, S)) * u).astype(np.float32)
    wgs = np.exp(0.3 * n((128, S))).astype(np.float32)
    page0 = (n((H, T2)) * u).astype(np.float32)
    d = (np.exp(0.3 * n(H)) / u[:, 0]).astype(np.float32)
    w2_words, w2_scales = pack_weight(n((H, H)) / np.sqrt(H) / u * u.T, "e2m1")
    b2 = (0.5 * n(H) * u[:, 0]).astype(np.float32)
    wgo = np.exp(0.3 * n((128, P))).astype(np.float32)
    offs = striped(np.random.permutation(T)[:S])
    offs2 = striped(np.random.permutation(T2)[:S])
    offs3 = striped(np.random.permutation(T2)[:P])
    offs4 = striped(np.random.permutation(T2)[:P])
    return {"tab_words": tab_words, "tab_scales": tab_scales, "offs": offs, "w1": w1, "b1": b1,
            "base": base, "wgs": wgs, "page0": page0, "offs2": offs2, "offs3": offs3, "d": d,
            "w2_words": w2_words, "w2_scales": w2_scales, "b2": b2, "wgo": wgo, "offs4": offs4}

def reference(tab_words, tab_scales, offs, w1, b1, base, wgs, page0, offs2, offs3, d,
              w2_words, w2_scales, b2, wgo, offs4):
    v = unpack_weight(tab_words, tab_scales, "e4m3")[:, unstriped(offs)]
    h = (mxq(f64(w1), 0, "e4m3").T @ v) + f64(b1)[:, None]
    h = np.maximum(h, f64(base))
    page = f64(page0).copy()
    page[:, unstriped(offs2)] = np.tile(f64(wgs), (H // 128, 1)) * h
    x = page[:, unstriped(offs3)]
    z = x * np.tanh(f64(d)[:, None] * x)
    w2 = unpack_weight(w2_words, w2_scales, "e2m1")
    y = np.abs(w2.T @ mxq(z, 0, "e4m3")) + f64(b2)[:, None]
    page[:, unstriped(offs4)] = np.tile(f64(wgo), (H // 128, 1)) * y
    return page

@@ -1,0 +1,271 @@
+from contextlib import ExitStack
+
+import concourse.mybir as mybir
+from concourse.masks import make_identity
+
+K, H, T, S, T2, E = 1024, 1024, 2048, 1024, 2048, 1024
+FLOPS = 2 * K * H * S + 2 * H * H * E
+
+F32 = mybir.dt.float32
+BF16 = mybir.dt.bfloat16
+I32 = mybir.dt.int32
+U32 = mybir.dt.uint32
+U16 = mybir.dt.uint16
+U8 = mybir.dt.uint8
+E4M3 = mybir.dt.float8_e4m3fn_x4
+E2M1 = mybir.dt.float4_e2m1fn_x4
+ALU = mybir.AluOpType
+ACT = mybir.ActivationFunctionType
+
+P = 128
+PASSES = 2
+TILES = H // P
+BANK = 512
+FIRST = 256
+W1_CHUNKS = [(0, 1), (1, 2), (2, 4), (4, 8)]
+
+
+def tile_list_frost_page_rewrite_kernel(
+    tc, tab_words, tab_scales, offs, w1, b1, base, wgs, page0, offs2, offs3, d,
+    w2_words, w2_scales, b2, wgo, offs4, out,
+):
+    nc = tc.nc
+    with ExitStack() as ctx:
+        lists = ctx.enter_context(tc.tile_pool(name="lists", bufs=1))
+        keep = ctx.enter_context(tc.tile_pool(name="keep", bufs=1))
+        ring = ctx.enter_context(tc.tile_pool(name="ring", bufs=2))
+        acc_pool = ctx.enter_context(tc.psum_pool(name="acc", bufs=4))
+        turn_pool = ctx.enter_context(tc.psum_pool(name="turn", bufs=2))
+
+        def load_list(name, src):
+            tile = lists.tile([P, S // 16], U16, name=name)
+            nc.sync.dma_start(tile[:], src)
+            return tile
+
+        def cols16(tile, lo, hi):
+            return tile[:, lo // 16 : hi // 16]
+
+        idx = load_list("idx", offs)
+        tab_sc = keep.tile([P, T], U8, name="tab_sc", align_bytes=64)
+        nc.vector.memset(tab_sc[:].bitcast(I32), 0)
+        for q in range(4):
+            nc.sync.dma_start(
+                tab_sc[32 * q : 32 * q + 8, :].bitcast(I32),
+                tab_scales[:, 4 * q : 4 * q + 4, :].bitcast(I32),
+            )
+        tab = []
+        for a in range(PASSES):
+            tile = keep.tile([P, T], I32, name="tab%d" % a, tag="big%d" % a, align_bytes=64)
+            nc.sync.dma_start(tile[:], tab_words[a].rearrange("p t i -> p (t i)").bitcast(I32))
+            tab.append(tile)
+
+        ident32 = keep.tile([P, P], F32, name="ident32")
+        ident16 = keep.tile([P, P], BF16, name="ident16")
+        vec_rows = keep.tile([P, P], F32, name="vec_rows")
+        nc.gpsimd.memset(vec_rows[:], 0.0)
+        make_identity(nc, ident32[:])
+        make_identity(nc, ident16[:])
+        for n, vec in enumerate((b1, d, b2)):
+            nc.sync.dma_start(vec_rows[TILES * n : TILES * (n + 1), :], vec.rearrange("(i p) -> i p", p=P))
+        vec_bank = turn_pool.tile([P, P], F32, name="vec_bank", tag="second")
+        nc.tensor.transpose(vec_bank[:], vec_rows[:], ident32[:])
+        vecs = keep.tile([P, 3 * TILES], F32, name="vecs")
+        nc.scalar.copy(vecs[:], vec_bank[:, 0 : 3 * TILES])
+
+        v_sc = keep.tile([P, S], U8, name="v_sc", align_bytes=64)
+        nc.vector.tensor_copy(v_sc[:], tab_sc[:].indirect(idx[:]))
+        v_codes = [keep.tile([P, S], U32, name="v_codes%d" % a, align_bytes=64) for a in range(PASSES)]
+        nc.vector.tensor_copy(v_codes[0][:], tab[0][:].bitcast(U32).indirect(idx[:]))
+        for lo in range(0, S, BANK):
+            nc.vector.tensor_copy(
+                v_codes[1][:, lo : lo + BANK], tab[1][:].bitcast(U32).indirect(cols16(idx, lo, lo + BANK))
+            )
+
+        w1_mx = {}
+
+        def quantise_w1(first, last):
+            n = last - first
+            woven = keep.tile([P, n, PASSES, P // 4, 4, 4], BF16, name="w1_woven%d" % first,
+                              tag="woven%d" % first, align_bytes=64)
+            for a in range(PASSES):
+                raw = keep.tile([P, 4, n * P], F32, name="w1_raw%d_%d" % (first, a),
+                                tag="raw%d_%d" % (first, a), align_bytes=64)
+                nc.sync.dma_start(
+                    raw[:],
+                    w1[512 * a : 512 * (a + 1), first * P : last * P].rearrange("(p j) c -> p j c", j=4),
+                )
+                nc.scalar.copy(
+                    woven[:, :, a].rearrange("p n c i j -> p n c j i"),
+                    raw[:].rearrange("p j (n c i) -> p n c j i", n=n, i=4),
+                )
+            codes = keep.tile([P, n * PASSES * P], U32, name="w1_codes%d" % first, align_bytes=64)
+            scales = keep.tile([P, n * PASSES * P], U8, name="w1_scales%d" % first, align_bytes=64)
+            nc.vector.quantize_mx(
+                codes[:].bitcast(E4M3), scales[:], woven[:].rearrange("p n a c i j -> p (n a c i j)")
+            )
+            for i in range(first, last):
+                for a in range(PASSES):
+                    lo = ((i - first) * PASSES + a) * P
+                    w1_mx[i, a] = (codes[:, lo : lo + P].bitcast(E4M3), scales[:, lo : lo + P])
+
+        pages = []
+        picked = {}
+        z_codes = {1: keep.tile([P, E], U32, name="z_codes1", align_bytes=64)}
+        z_sc = [keep.tile([P, E], U8, name="z_sc%d" % a, align_bytes=64) for a in range(PASSES)]
+        held = {}
+
+        def first_stage(i):
+            base_i = keep.tile([P, S], F32, name="base%d" % i, tag="base%d" % (i % 4), align_bytes=64)
+            nc.sync.dma_start(base_i[:], base[i * P : (i + 1) * P, :])
+            if i == 0:
+                held["wgs"] = keep.tile([P, S], F32, name="wgs_sb")
+                nc.sync.dma_start(held["wgs"][:], wgs)
+                held["idx2"] = load_list("idx2", offs2)
+            page = keep.tile([P, T2], F32, name="page%d" % i)
+            nc.sync.dma_start(page[:], page0[i * P : (i + 1) * P, :])
+            pages.append(page)
+            if i == 0:
+                held["idx3"] = load_list("idx3", offs3)
+            h = keep.tile([P, S], F32, name="h%d" % i, tag="h", align_bytes=64)
+            for lo in range(0, S, BANK):
+                acc = acc_pool.tile([P, BANK], F32, name="acc")
+                for a in range(PASSES):
+                    nc.tensor.matmul_mx(
+                        acc[:], lhsT=w1_mx[i, a][0], lhsT_scale=w1_mx[i, a][1],
+                        rhs=v_codes[a][:, lo : lo + BANK].bitcast(E4M3),
+                        rhs_scale=v_sc[4 * a :, lo : lo + BANK],
+                        start=(a == 0), stop=(a == PASSES - 1),
+                    )
+                nc.vector.scalar_tensor_tensor(
+                    h[:, lo : lo + BANK], acc[:], vecs[:, i : i + 1], base_i[:, lo : lo + BANK], ALU.add, ALU.max
+                )
+            if i >= 2:
+                z = keep.tile([P, E], BF16, name="z%d" % (i - 2), tag="base%d" % (i % 4), align_bytes=64)
+                turn(i - 2, 0, E, z[:], nc.vector)
+            nc.vector.tensor_tensor(page[:].indirect(held["idx2"][:]), h[:], held["wgs"][:], ALU.mult)
+
+        def pick(i, lo, hi, x, th):
+            nc.vector.tensor_copy(x, pages[i][:].indirect(cols16(held["idx3"], lo, hi)))
+            nc.scalar.activation(th, x, ACT.Tanh, scale=vecs[:, TILES + i : TILES + i + 1])
+            picked[i, lo, hi] = (x, th)
+
+        z_turned = {(0, 0): keep.tile([P, E // P, 2, P], F32, name="zt0", align_bytes=64)}
+
+        def turn(i, lo, hi, z, engine):
+            x, th = picked[i, lo, hi]
+            engine.tensor_tensor(z, x, th, ALU.mult)
+            groups = (hi - lo) // P
+            bank = turn_pool.tile([P, groups, P], BF16, name="first")
+            for g in range(groups):
+                nc.tensor.transpose(bank[:, g, :], z[:, g * P : (g + 1) * P], ident16[:])
+            words = bank[:].bitcast(F32).rearrange("p g (m e) -> p g e m", e=2)
+            a, u = divmod(i, 4)
+            cuts = [lo, hi] if (a == 0 or lo > 0 or hi == FIRST) else [lo, FIRST, hi]
+            for c0, c1 in zip(cuts, cuts[1:]):
+                nc.scalar.copy(
+                    z_turned[a, c0][:, :, :, 32 * u : 32 * (u + 1)],
+                    words[:, (c0 - lo) // P : (c1 - lo) // P],
+                )
+
+        def quantise_z(a, lo, hi, tag, widths):
+            woven = keep.tile([P, (hi - lo) * 4], BF16, name="z_woven%d_%d" % (a, lo), tag=tag, align_bytes=64)
+            words = woven[:].bitcast(F32)
+            for g0 in range(0, (hi - lo) // P, 2):
+                bank = turn_pool.tile([P, 2, 2, P], F32, name="second", tag="second")
+                for g in range(2):
+                    for e in range(2):
+                        nc.tensor.transpose(bank[:, g, e, :], z_turned[a, lo][:, g0 + g, e, :], ident32[:])
+                nc.scalar.copy(
+                    words[:, g0 * 2 * P : (g0 + 2) * 2 * P].rearrange("p (g j e) -> p g j e", g=2, e=2),
+                    bank[:].rearrange("p g e j -> p g j e"),
+                )
+            c0 = lo
+            for width in widths:
+                nc.vector.quantize_mx(
+                    z_codes[a][:, c0 : c0 + width].bitcast(E4M3), z_sc[a][:, c0 : c0 + width],
+                    woven[:, (c0 - lo) * 4 : (c0 - lo + width) * 4],
+                )
+                c0 = c0 + width
+
+        starts = dict(W1_CHUNKS)
+        last = TILES - 1
+        x_tags = {0: "woven1", 1: "woven2", 3: "woven4", 4: "woven1", 5: "woven2"}
+        quantise_w1(0, starts[0])
+        for i in range(TILES):
+            if i == 6:
+                z_turned[1, 0] = keep.tile([P, FIRST // P, 2, P], F32, name="zt1a", tag="raw2_0", align_bytes=64)
+                z_turned[1, FIRST] = keep.tile(
+                    [P, (E - FIRST) // P, 2, P], F32, name="zt1b", tag="raw4_1", align_bytes=64
+                )
+            first_stage(i)
+            if i + 1 in starts:
+                quantise_w1(i + 1, starts[i + 1])
+            if i == last:
+                pick(i, 0, FIRST, keep.tile([P, FIRST], F32, name="x_last_a", tag="x_last")[:],
+                     ring.tile([P, FIRST], F32, name="th")[:])
+                z = keep.tile([P, FIRST], BF16, name="z%d" % (i - 1), tag="h", align_bytes=64)
+                turn(i - 1, 0, FIRST, z[:], nc.vector)
+            if i == 6:
+                z_codes[0] = keep.tile([P, E], U32, name="z_codes0", tag="base2", align_bytes=64)
+                quantise_z(0, 0, E, "big0", [E])
+            if i < last:
+                hi = FIRST if i == last - 1 else E
+                if i in x_tags:
+                    x = keep.tile([P, hi], F32, name="x%d" % i, tag=x_tags[i], align_bytes=64)
+                else:
+                    x = ring.tile([P, hi], F32, name="x")
+                pick(i, 0, hi, x[:], ring.tile([P, hi], F32, name="th")[:])
+
+        w2 = keep.tile([P, PASSES, 2 * H], U8, name="w2", align_bytes=64)
+        nc.sync.dma_start(w2[:].bitcast(I32), w2_words.rearrange("a p n -> p a n").bitcast(I32))
+        w2_sc = keep.tile([P, PASSES, H], U8, name="w2_sc", align_bytes=64)
+        nc.gpsimd.memset(w2_sc[:].bitcast(I32), 0)
+        for q in range(4):
+            nc.sync.dma_start(
+                w2_sc[32 * q : 32 * q + 4].bitcast(I32),
+                w2_scales[:, 4 * q : 4 * q + 4, :].rearrange("a r n -> r a n").bitcast(I32),
+            )
+        wgo_sb = keep.tile([P, E], F32, name="wgo_sb")
+        nc.sync.dma_start(wgo_sb[:], wgo)
+        idx4 = load_list("idx4", offs4)
+
+        z_last_a = keep.tile([P, FIRST], BF16, name="z_last_a", align_bytes=64)
+        turn(last, 0, FIRST, z_last_a[:], nc.vector)
+        quantise_z(1, 0, FIRST, "woven_a", [FIRST])
+        x_rest = keep.tile([P, 2, E - FIRST], F32, name="x_rest", tag="x_last")
+        th_rest = keep.tile([P, 2, E - FIRST], F32, name="th_rest", tag="raw2_0", align_bytes=64)
+        pick(last - 1, FIRST, E, x_rest[:, 0, :], th_rest[:, 0, :])
+        pick(last, FIRST, E, x_rest[:, 1, :], th_rest[:, 1, :])
+        z_rest = keep.tile([P, 2, E - FIRST], BF16, name="z_rest", tag="woven_a", align_bytes=64)
+        turn(last - 1, FIRST, E, z_rest[:, 0, :], nc.vector)
+        turn(last, FIRST, E, z_rest[:, 1, :], nc.vector)
+
+        def second_stage(n, lo, hi, cuts, tag, bufs):
+            y = ring.tile([P, hi - lo], F32, name="y", tag=tag, bufs=bufs)
+            for c0, c1 in zip(cuts, cuts[1:]):
+                acc = acc_pool.tile([P, c1 - c0], F32, name="acc")
+                for a in range(PASSES):
+                    nc.tensor.matmul_mx(
+                        acc[:], lhsT=w2[:, a, 2 * P * n : 2 * P * (n + 1)].bitcast(E2M1),
+                        lhsT_scale=w2_sc[:, a, P * n : P * (n + 1)],
+                        rhs=z_codes[a][:, c0:c1].bitcast(E4M3), rhs_scale=z_sc[a][:, c0:c1],
+                        start=(a == 0), stop=(a == PASSES - 1),
+                    )
+                mag = ring.tile([P, c1 - c0], F32, name="mag")
+                nc.scalar.activation(mag[:], acc[:], ACT.Abs)
+                nc.scalar.activation(
+                    y[:, c0 - lo : c1 - lo], mag[:], ACT.Identity, bias=vecs[:, 2 * TILES + n : 2 * TILES + n + 1]
+                )
+            nc.vector.tensor_tensor(pages[n][:].indirect(cols16(idx4, lo, hi)), y[:], wgo_sb[:, lo:hi], ALU.mult)
+
+        early = 6
+        second_stage(0, 0, FIRST, [0, FIRST], "y_first", 3)
+        quantise_z(1, FIRST, E, "big1", [FIRST, BANK])
+        for n in range(1, early):
+            second_stage(n, 0, FIRST, [0, FIRST], "y_first", 3)
+        for n in range(TILES):
+            if n < early:
+                second_stage(n, FIRST, E, [FIRST, BANK, E], "x", 2)
+            else:
+                second_stage(n, 0, E, [0, BANK, E], "x", 2)
+            nc.sync.dma_start(out[n * P : (n + 1) * P, :], pages[n][:])

@@ -61,16 +61,21 @@ def tile_list_frost_page_rewrite_kernel(
 
         ident32 = keep.tile([P, P], F32, name="ident32")
         ident16 = keep.tile([P, P], BF16, name="ident16")
-        vec_rows = keep.tile([P, P], F32, name="vec_rows")
-        nc.gpsimd.memset(vec_rows[:], 0.0)
+
+        def load_vectors(name, vectors):
+            rows = keep.tile([P, P], F32, name=name + "_rows")
+            nc.gpsimd.memset(rows[:], 0.0)
+            for n, vec in enumerate(vectors):
+                nc.sync.dma_start(rows[TILES * n : TILES * (n + 1), :], vec.rearrange("(i p) -> i p", p=P))
+            bank = turn_pool.tile([P, P], F32, name=name + "_bank", tag="second")
+            nc.tensor.transpose(bank[:], rows[:], ident32[:])
+            cols = keep.tile([P, len(vectors) * TILES], F32, name=name + "_cols")
+            nc.scalar.copy(cols[:], bank[:, 0 : len(vectors) * TILES])
+            return cols
+
         make_identity(nc, ident32[:])
         make_identity(nc, ident16[:])
-        for n, vec in enumerate((b1, d, b2)):
-            nc.sync.dma_start(vec_rows[TILES * n : TILES * (n + 1), :], vec.rearrange("(i p) -> i p", p=P))
-        vec_bank = turn_pool.tile([P, P], F32, name="vec_bank", tag="second")
-        nc.tensor.transpose(vec_bank[:], vec_rows[:], ident32[:])
-        vecs = keep.tile([P, 3 * TILES], F32, name="vecs")
-        nc.scalar.copy(vecs[:], vec_bank[:, 0 : 3 * TILES])
+        b1_cols = load_vectors("b1", [b1])
 
         v_sc = keep.tile([P, S], U8, name="v_sc", align_bytes=64)
         nc.vector.tensor_copy(v_sc[:], tab_sc[:].indirect(idx[:]))
@@ -82,8 +87,9 @@ def tile_list_frost_page_rewrite_kernel(
             )
 
         w1_mx = {}
+        held = {}
 
-        def quantise_w1(first, last):
+        def weave_w1(first, last):
             n = last - first
             woven = keep.tile([P, n, PASSES, P // 4, 4, 4], BF16, name="w1_woven%d" % first,
                               tag="woven%d" % first, align_bytes=64)
@@ -98,7 +104,12 @@ def tile_list_frost_page_rewrite_kernel(
                     woven[:, :, a].rearrange("p n c i j -> p n c j i"),
                     raw[:].rearrange("p j (n c i) -> p n c j i", n=n, i=4),
                 )
-            codes = keep.tile([P, n * PASSES * P], U32, name="w1_codes%d" % first, align_bytes=64)
+            held["woven", first] = woven
+
+        def quantise_w1(first, last, tag):
+            n = last - first
+            woven = held["woven", first]
+            codes = keep.tile([P, n * PASSES * P], U32, name="w1_codes%d" % first, tag=tag, align_bytes=64)
             scales = keep.tile([P, n * PASSES * P], U8, name="w1_scales%d" % first, align_bytes=64)
             nc.vector.quantize_mx(
                 codes[:].bitcast(E4M3), scales[:], woven[:].rearrange("p n a c i j -> p (n a c i j)")
@@ -112,10 +123,10 @@ def tile_list_frost_page_rewrite_kernel(
         picked = {}
         z_codes = {1: keep.tile([P, E], U32, name="z_codes1", align_bytes=64)}
         z_sc = [keep.tile([P, E], U8, name="z_sc%d" % a, align_bytes=64) for a in range(PASSES)]
-        held = {}
+        base_tags = ["base0", "base1", "base2", "base3", "base0", "base2", "base6", "base0"]
 
         def first_stage(i):
-            base_i = keep.tile([P, S], F32, name="base%d" % i, tag="base%d" % (i % 4), align_bytes=64)
+            base_i = keep.tile([P, S], F32, name="base%d" % i, tag=base_tags[i], align_bytes=64)
             nc.sync.dma_start(base_i[:], base[i * P : (i + 1) * P, :])
             if i == 0:
                 held["wgs"] = keep.tile([P, S], F32, name="wgs_sb")
@@ -126,7 +137,8 @@ def tile_list_frost_page_rewrite_kernel(
             pages.append(page)
             if i == 0:
                 held["idx3"] = load_list("idx3", offs3)
-            h = keep.tile([P, S], F32, name="h%d" % i, tag="h", align_bytes=64)
+                held["vecs"] = load_vectors("d_b2", [d, b2])
+            h = keep.tile([P, S], F32, name="h%d" % i, tag="h%d" % (i % 2), align_bytes=64)
             for lo in range(0, S, BANK):
                 acc = acc_pool.tile([P, BANK], F32, name="acc")
                 for a in range(PASSES):
@@ -137,16 +149,18 @@ def tile_list_frost_page_rewrite_kernel(
                         start=(a == 0), stop=(a == PASSES - 1),
                     )
                 nc.vector.scalar_tensor_tensor(
-                    h[:, lo : lo + BANK], acc[:], vecs[:, i : i + 1], base_i[:, lo : lo + BANK], ALU.add, ALU.max
+                    h[:, lo : lo + BANK], acc[:], b1_cols[:, i : i + 1], base_i[:, lo : lo + BANK], ALU.add, ALU.max
                 )
-            if i >= 2:
-                z = keep.tile([P, E], BF16, name="z%d" % (i - 2), tag="base%d" % (i % 4), align_bytes=64)
-                turn(i - 2, 0, E, z[:], nc.vector)
+            if i in (1, 3):
+                quantise_w1(i + 1, starts[i + 1], base_tags[i])
+            if i == 6:
+                z_codes[0] = keep.tile([P, E], U32, name="z_codes0", tag=base_tags[i], align_bytes=64)
+                quantise_z(0, 0, E, "big0", 0)
             nc.vector.tensor_tensor(page[:].indirect(held["idx2"][:]), h[:], held["wgs"][:], ALU.mult)
 
         def pick(i, lo, hi, x, th):
             nc.vector.tensor_copy(x, pages[i][:].indirect(cols16(held["idx3"], lo, hi)))
-            nc.scalar.activation(th, x, ACT.Tanh, scale=vecs[:, TILES + i : TILES + i + 1])
+            nc.scalar.activation(th, x, ACT.Tanh, scale=held["vecs"][:, i : i + 1])
             picked[i, lo, hi] = (x, th)
 
         z_turned = {(0, 0): keep.tile([P, E // P, 2, P], F32, name="zt0", align_bytes=64)}
@@ -167,56 +181,59 @@ def tile_list_frost_page_rewrite_kernel(
                     words[:, (c0 - lo) // P : (c1 - lo) // P],
                 )
 
-        def quantise_z(a, lo, hi, tag, widths):
+        def quantise_z(a, lo, hi, tag, held_from):
             woven = keep.tile([P, (hi - lo) * 4], BF16, name="z_woven%d_%d" % (a, lo), tag=tag, align_bytes=64)
             words = woven[:].bitcast(F32)
             for g0 in range(0, (hi - lo) // P, 2):
                 bank = turn_pool.tile([P, 2, 2, P], F32, name="second", tag="second")
                 for g in range(2):
                     for e in range(2):
-                        nc.tensor.transpose(bank[:, g, e, :], z_turned[a, lo][:, g0 + g, e, :], ident32[:])
+                        nc.tensor.transpose(bank[:, g, e, :], z_turned[a, held_from][:, (lo - held_from) // P + g0 + g, e, :], ident32[:])
                 nc.scalar.copy(
                     words[:, g0 * 2 * P : (g0 + 2) * 2 * P].rearrange("p (g j e) -> p g j e", g=2, e=2),
                     bank[:].rearrange("p g e j -> p g j e"),
                 )
-            c0 = lo
-            for width in widths:
-                nc.vector.quantize_mx(
-                    z_codes[a][:, c0 : c0 + width].bitcast(E4M3), z_sc[a][:, c0 : c0 + width],
-                    woven[:, (c0 - lo) * 4 : (c0 - lo + width) * 4],
-                )
-                c0 = c0 + width
+            nc.vector.quantize_mx(z_codes[a][:, lo:hi].bitcast(E4M3), z_sc[a][:, lo:hi], woven[:])
 
         starts = dict(W1_CHUNKS)
         last = TILES - 1
-        x_tags = {0: "woven1", 1: "woven2", 3: "woven4", 4: "woven1", 5: "woven2"}
-        quantise_w1(0, starts[0])
+        th_tags = {0: "raw2_1", 2: "raw4_1"}
+        weave_w1(0, 1)
+        quantise_w1(0, 1, "codes0")
         for i in range(TILES):
-            if i == 6:
+            if i == 5:
                 z_turned[1, 0] = keep.tile([P, FIRST // P, 2, P], F32, name="zt1a", tag="raw2_0", align_bytes=64)
                 z_turned[1, FIRST] = keep.tile(
                     [P, (E - FIRST) // P, 2, P], F32, name="zt1b", tag="raw4_1", align_bytes=64
                 )
             first_stage(i)
-            if i + 1 in starts:
-                quantise_w1(i + 1, starts[i + 1])
+            if i == 0:
+                weave_w1(1, 2)
+                quantise_w1(1, 2, "codes1")
+                weave_w1(2, 4)
+            if i == 2:
+                weave_w1(4, 8)
+            if 0 < i < last:
+                z = keep.tile([P, E], BF16, name="z%d" % (i - 1), tag="h%d" % (i % 2), align_bytes=64)
+                turn(i - 1, 0, E, z[:], nc.gpsimd)
             if i == last:
                 pick(i, 0, FIRST, keep.tile([P, FIRST], F32, name="x_last_a", tag="x_last")[:],
                      ring.tile([P, FIRST], F32, name="th")[:])
-                z = keep.tile([P, FIRST], BF16, name="z%d" % (i - 1), tag="h", align_bytes=64)
+                z = keep.tile([P, FIRST], BF16, name="z%d" % (i - 1), tag="h%d" % (i % 2), align_bytes=64)
                 turn(i - 1, 0, FIRST, z[:], nc.vector)
-            if i == 6:
-                z_codes[0] = keep.tile([P, E], U32, name="z_codes0", tag="base2", align_bytes=64)
-                quantise_z(0, 0, E, "big0", [E])
             if i < last:
                 hi = FIRST if i == last - 1 else E
-                if i in x_tags:
-                    x = keep.tile([P, hi], F32, name="x%d" % i, tag=x_tags[i], align_bytes=64)
+                if i == 0:
+                    x = keep.tile([P, hi], F32, name="x0", tag="woven1", align_bytes=64)
                 else:
-                    x = ring.tile([P, hi], F32, name="x")
-                pick(i, 0, hi, x[:], ring.tile([P, hi], F32, name="th")[:])
+                    x = ring.tile([P, hi], F32, name="x", align_bytes=64)
+                if i in th_tags:
+                    th = keep.tile([P, hi], F32, name="th%d" % i, tag=th_tags[i], align_bytes=64)
+                else:
+                    th = ring.tile([P, hi], F32, name="th")
+                pick(i, 0, hi, x[:], th[:])
 
-        w2 = keep.tile([P, PASSES, 2 * H], U8, name="w2", align_bytes=64)
+        w2 = keep.tile([P, PASSES, 2 * H], U8, name="w2", tag="woven4", align_bytes=64)
         nc.sync.dma_start(w2[:].bitcast(I32), w2_words.rearrange("a p n -> p a n").bitcast(I32))
         w2_sc = keep.tile([P, PASSES, H], U8, name="w2_sc", align_bytes=64)
         nc.gpsimd.memset(w2_sc[:].bitcast(I32), 0)
@@ -225,13 +242,13 @@ def tile_list_frost_page_rewrite_kernel(
                 w2_sc[32 * q : 32 * q + 4].bitcast(I32),
                 w2_scales[:, 4 * q : 4 * q + 4, :].rearrange("a r n -> r a n").bitcast(I32),
             )
-        wgo_sb = keep.tile([P, E], F32, name="wgo_sb")
+        wgo_sb = keep.tile([P, E], F32, name="wgo_sb", tag="woven2", align_bytes=64)
         nc.sync.dma_start(wgo_sb[:], wgo)
         idx4 = load_list("idx4", offs4)
 
         z_last_a = keep.tile([P, FIRST], BF16, name="z_last_a", align_bytes=64)
         turn(last, 0, FIRST, z_last_a[:], nc.vector)
-        quantise_z(1, 0, FIRST, "woven_a", [FIRST])
+        quantise_z(1, 0, FIRST, "woven_a", 0)
         x_rest = keep.tile([P, 2, E - FIRST], F32, name="x_rest", tag="x_last")
         th_rest = keep.tile([P, 2, E - FIRST], F32, name="th_rest", tag="raw2_0", align_bytes=64)
         pick(last - 1, FIRST, E, x_rest[:, 0, :], th_rest[:, 0, :])
@@ -241,7 +258,7 @@ def tile_list_frost_page_rewrite_kernel(
         turn(last, FIRST, E, z_rest[:, 1, :], nc.vector)
 
         def second_stage(n, lo, hi, cuts, tag, bufs):
-            y = ring.tile([P, hi - lo], F32, name="y", tag=tag, bufs=bufs)
+            y = (keep if bufs == 1 else ring).tile([P, hi - lo], F32, name="y", tag=tag, bufs=bufs, align_bytes=64)
             for c0, c1 in zip(cuts, cuts[1:]):
                 acc = acc_pool.tile([P, c1 - c0], F32, name="acc")
                 for a in range(PASSES):
@@ -254,15 +271,17 @@ def tile_list_frost_page_rewrite_kernel(
                 mag = ring.tile([P, c1 - c0], F32, name="mag")
                 nc.scalar.activation(mag[:], acc[:], ACT.Abs)
                 nc.scalar.activation(
-                    y[:, c0 - lo : c1 - lo], mag[:], ACT.Identity, bias=vecs[:, 2 * TILES + n : 2 * TILES + n + 1]
+                    y[:, c0 - lo : c1 - lo], mag[:], ACT.Identity, bias=held["vecs"][:, TILES + n : TILES + n + 1]
                 )
             nc.vector.tensor_tensor(pages[n][:].indirect(cols16(idx4, lo, hi)), y[:], wgo_sb[:, lo:hi], ALU.mult)
 
         early = 6
         second_stage(0, 0, FIRST, [0, FIRST], "y_first", 3)
-        quantise_z(1, FIRST, E, "big1", [FIRST, BANK])
+        quantise_z(1, FIRST, BANK, "h0", FIRST)
+        quantise_z(1, BANK, E, "big1", FIRST)
         for n in range(1, early):
-            second_stage(n, 0, FIRST, [0, FIRST], "y_first", 3)
+            tag = {early - 2: "h0", early - 1: "big1"}.get(n, "y_first")
+            second_stage(n, 0, FIRST, [0, FIRST], tag, 3 if tag == "y_first" else 1)
         for n in range(TILES):
             if n < early:
                 second_stage(n, FIRST, E, [FIRST, BANK, E], "x", 2)

@@ -22,7 +22,7 @@ PASSES = 2
 TILES = H // P
 BANK = 512
 FIRST = 256
-W1_CHUNKS = [(0, 1), (1, 2), (2, 4), (4, 8)]
+FUSED = 2
 
 
 def tile_list_frost_page_rewrite_kernel(
@@ -53,11 +53,13 @@ def tile_list_frost_page_rewrite_kernel(
                 tab_sc[32 * q : 32 * q + 8, :].bitcast(I32),
                 tab_scales[:, 4 * q : 4 * q + 4, :].bitcast(I32),
             )
-        tab = []
-        for a in range(PASSES):
+
+        def load_table(a):
             tile = keep.tile([P, T], I32, name="tab%d" % a, tag="big%d" % a, align_bytes=64)
             nc.sync.dma_start(tile[:], tab_words[a].rearrange("p t i -> p (t i)").bitcast(I32))
-            tab.append(tile)
+            return tile
+
+        tab0 = load_table(0)
 
         ident32 = keep.tile([P, P], F32, name="ident32")
         ident16 = keep.tile([P, P], BF16, name="ident16")
@@ -75,16 +77,11 @@ def tile_list_frost_page_rewrite_kernel(
 
         make_identity(nc, ident32[:])
         make_identity(nc, ident16[:])
-        b1_cols = load_vectors("b1", [b1])
 
         v_sc = keep.tile([P, S], U8, name="v_sc", align_bytes=64)
         nc.vector.tensor_copy(v_sc[:], tab_sc[:].indirect(idx[:]))
         v_codes = [keep.tile([P, S], U32, name="v_codes%d" % a, align_bytes=64) for a in range(PASSES)]
-        nc.vector.tensor_copy(v_codes[0][:], tab[0][:].bitcast(U32).indirect(idx[:]))
-        for lo in range(0, S, BANK):
-            nc.vector.tensor_copy(
-                v_codes[1][:, lo : lo + BANK], tab[1][:].bitcast(U32).indirect(cols16(idx, lo, lo + BANK))
-            )
+        nc.vector.tensor_copy(v_codes[0][:], tab0[:].bitcast(U32).indirect(idx[:]))
 
         w1_mx = {}
         held = {}
@@ -109,8 +106,8 @@ def tile_list_frost_page_rewrite_kernel(
         def quantise_w1(first, last, tag):
             n = last - first
             woven = held["woven", first]
-            codes = keep.tile([P, n * PASSES * P], U32, name="w1_codes%d" % first, tag=tag, align_bytes=64)
-            scales = keep.tile([P, n * PASSES * P], U8, name="w1_scales%d" % first, align_bytes=64)
+            codes = keep.tile([P, n * PASSES * P], U32, name="w1_codes%d" % first, align_bytes=64)
+            scales = keep.tile([P, n * PASSES * P], U8, name="w1_scales%d" % first, tag=tag, align_bytes=64)
             nc.vector.quantize_mx(
                 codes[:].bitcast(E4M3), scales[:], woven[:].rearrange("p n a c i j -> p (n a c i j)")
             )
@@ -122,24 +119,17 @@ def tile_list_frost_page_rewrite_kernel(
         pages = []
         picked = {}
         z_codes = {1: keep.tile([P, E], U32, name="z_codes1", align_bytes=64)}
+        feats = {}
         z_sc = [keep.tile([P, E], U8, name="z_sc%d" % a, align_bytes=64) for a in range(PASSES)]
-        base_tags = ["base0", "base1", "base2", "base3", "base0", "base2", "base6", "base0"]
 
-        def first_stage(i):
-            base_i = keep.tile([P, S], F32, name="base%d" % i, tag=base_tags[i], align_bytes=64)
+        def load_base(i):
+            base_i = ring.tile([P, S], F32, name="base_i", bufs=3)
             nc.sync.dma_start(base_i[:], base[i * P : (i + 1) * P, :])
-            if i == 0:
-                held["wgs"] = keep.tile([P, S], F32, name="wgs_sb")
-                nc.sync.dma_start(held["wgs"][:], wgs)
-                held["idx2"] = load_list("idx2", offs2)
-            page = keep.tile([P, T2], F32, name="page%d" % i)
-            nc.sync.dma_start(page[:], page0[i * P : (i + 1) * P, :])
-            pages.append(page)
-            if i == 0:
-                held["idx3"] = load_list("idx3", offs3)
-                held["vecs"] = load_vectors("d_b2", [d, b2])
-            h = keep.tile([P, S], F32, name="h%d" % i, tag="h%d" % (i % 2), align_bytes=64)
-            for lo in range(0, S, BANK):
+            return base_i
+
+        def features(i, base_i, h, first, end):
+            feats[i, first] = h
+            for lo in range(first, end, BANK):
                 acc = acc_pool.tile([P, BANK], F32, name="acc")
                 for a in range(PASSES):
                     nc.tensor.matmul_mx(
@@ -149,14 +139,23 @@ def tile_list_frost_page_rewrite_kernel(
                         start=(a == 0), stop=(a == PASSES - 1),
                     )
                 nc.vector.scalar_tensor_tensor(
-                    h[:, lo : lo + BANK], acc[:], b1_cols[:, i : i + 1], base_i[:, lo : lo + BANK], ALU.add, ALU.max
+                    h[:, lo - first : lo - first + BANK], acc[:], held["b1"][:, i : i + 1], base_i[:, lo : lo + BANK],
+                    ALU.add, ALU.max,
                 )
-            if i in (1, 3):
-                quantise_w1(i + 1, starts[i + 1], base_tags[i])
-            if i == 6:
-                z_codes[0] = keep.tile([P, E], U32, name="z_codes0", tag=base_tags[i], align_bytes=64)
-                quantise_z(0, 0, E, "big0", 0)
-            nc.vector.tensor_tensor(page[:].indirect(held["idx2"][:]), h[:], held["wgs"][:], ALU.mult)
+            if i >= FUSED:
+                nc.gpsimd.tensor_tensor(h[:], h[:], held["wgs"][:], ALU.mult)
+
+        def load_page(i):
+            page = keep.tile([P, T2], F32, name="page%d" % i)
+            nc.sync.dma_start(page[:], page0[i * P : (i + 1) * P, :])
+            pages.append(page)
+
+        def place(i, lo, hi):
+            window = pages[i][:].indirect(cols16(held["idx2"], lo, hi))
+            if i >= FUSED:
+                nc.vector.tensor_copy(window, feats[i, lo][:])
+            else:
+                nc.vector.tensor_tensor(window, feats[i, lo][:], held["wgs"][:, lo:hi], ALU.mult)
 
         def pick(i, lo, hi, x, th):
             nc.vector.tensor_copy(x, pages[i][:].indirect(cols16(held["idx3"], lo, hi)))
@@ -195,43 +194,71 @@ def tile_list_frost_page_rewrite_kernel(
                 )
             nc.vector.quantize_mx(z_codes[a][:, lo:hi].bitcast(E4M3), z_sc[a][:, lo:hi], woven[:])
 
-        starts = dict(W1_CHUNKS)
         last = TILES - 1
-        th_tags = {0: "raw2_1", 2: "raw4_1"}
         weave_w1(0, 1)
-        quantise_w1(0, 1, "codes0")
-        for i in range(TILES):
-            if i == 5:
+        quantise_w1(0, 1, "scales0")
+        tab1 = load_table(1)
+        for lo in range(0, S, BANK):
+            nc.vector.tensor_copy(
+                v_codes[1][:, lo : lo + BANK], tab1[:].bitcast(U32).indirect(cols16(idx, lo, lo + BANK))
+            )
+        held["b1"] = load_vectors("b1", [b1])
+        base0 = load_base(0)
+        features(0, base0, keep.tile([P, BANK], F32, name="h0a", tag="h0", align_bytes=64), 0, BANK)
+        held["wgs"] = keep.tile([P, S], F32, name="wgs_sb")
+        nc.sync.dma_start(held["wgs"][:], wgs)
+        held["idx2"] = load_list("idx2", offs2)
+        load_page(0)
+        place(0, 0, BANK)
+        weave_w1(1, 2)
+        quantise_w1(1, 2, "scales1")
+        features(0, base0, keep.tile([P, BANK], F32, name="h0b", tag="woven1", align_bytes=64), BANK, S)
+        place(0, BANK, S)
+        features(1, load_base(1), keep.tile([P, S], F32, name="h1", tag="raw0_0", align_bytes=64), 0, S)
+        weave_w1(2, 4)
+        quantise_w1(2, 4, "scales2")
+        held["idx3"] = load_list("idx3", offs3)
+        held["vecs"] = load_vectors("d_b2", [d, b2])
+        x0 = keep.tile([P, E], F32, name="x0", tag="woven2", align_bytes=64)
+        features(2, load_base(2), keep.tile([P, S], F32, name="h2", tag="h0", align_bytes=64), 0, S)
+        weave_w1(4, 8)
+        load_page(1)
+        pick(0, 0, E, x0[:], keep.tile([P, E], F32, name="th0", tag="raw4_1", align_bytes=64)[:])
+        for i in range(1, TILES):
+            if i > 1:
+                load_page(i)
+            place(i, 0, S)
+            if i == 1:
+                quantise_w1(4, 8, "raw0_0")
+            if i == 4:
                 z_turned[1, 0] = keep.tile([P, FIRST // P, 2, P], F32, name="zt1a", tag="raw2_0", align_bytes=64)
                 z_turned[1, FIRST] = keep.tile(
                     [P, (E - FIRST) // P, 2, P], F32, name="zt1b", tag="raw4_1", align_bytes=64
                 )
-            first_stage(i)
-            if i == 0:
-                weave_w1(1, 2)
-                quantise_w1(1, 2, "codes1")
-                weave_w1(2, 4)
-            if i == 2:
-                weave_w1(4, 8)
-            if 0 < i < last:
-                z = keep.tile([P, E], BF16, name="z%d" % (i - 1), tag="h%d" % (i % 2), align_bytes=64)
-                turn(i - 1, 0, E, z[:], nc.gpsimd)
             if i == last:
                 pick(i, 0, FIRST, keep.tile([P, FIRST], F32, name="x_last_a", tag="x_last")[:],
                      ring.tile([P, FIRST], F32, name="th")[:])
                 z = keep.tile([P, FIRST], BF16, name="z%d" % (i - 1), tag="h%d" % (i % 2), align_bytes=64)
                 turn(i - 1, 0, FIRST, z[:], nc.vector)
-            if i < last:
+            else:
+                if i == 1:
+                    z = keep.tile([P, E], BF16, name="z0", tag="woven4", align_bytes=64)
+                    turn(0, 0, E, z[:], nc.gpsimd)
                 hi = FIRST if i == last - 1 else E
-                if i == 0:
-                    x = keep.tile([P, hi], F32, name="x0", tag="woven1", align_bytes=64)
+                if i == 4:
+                    x = keep.tile([P, hi], F32, name="x4", tag="zc0", align_bytes=64)
                 else:
                     x = ring.tile([P, hi], F32, name="x", align_bytes=64)
-                if i in th_tags:
-                    th = keep.tile([P, hi], F32, name="th%d" % i, tag=th_tags[i], align_bytes=64)
-                else:
-                    th = ring.tile([P, hi], F32, name="th")
-                pick(i, 0, hi, x[:], th[:])
+                pick(i, 0, hi, x[:], ring.tile([P, hi], F32, name="th")[:])
+                if i + 2 < TILES:
+                    h = keep.tile([P, S], F32, name="h%d" % (i + 2), tag="h%d" % (i % 2), align_bytes=64)
+                    features(i + 2, load_base(i + 2), h, 0, S)
+                if i < last - 1:
+                    z = ring.tile([P, E], BF16, name="z", align_bytes=64)
+                    turn(i, 0, E, z[:], nc.gpsimd)
+                if i == 4:
+                    z_codes[0] = keep.tile([P, E], U32, name="z_codes0", tag="zc0", align_bytes=64)
+                    quantise_z(0, 0, E, "big0", 0)
 
         w2 = keep.tile([P, PASSES, 2 * H], U8, name="w2", tag="woven4", align_bytes=64)
         nc.sync.dma_start(w2[:].bitcast(I32), w2_words.rearrange("a p n -> p a n").bitcast(I32))

from contextlib import ExitStack

import concourse.mybir as mybir
from concourse.masks import make_identity

K, H, T, S, T2, E = 1024, 1024, 2048, 1024, 2048, 1024
FLOPS = 2 * K * H * S + 2 * H * H * E

F32 = mybir.dt.float32
BF16 = mybir.dt.bfloat16
I32 = mybir.dt.int32
U32 = mybir.dt.uint32
U16 = mybir.dt.uint16
U8 = mybir.dt.uint8
E4M3 = mybir.dt.float8_e4m3fn_x4
E2M1 = mybir.dt.float4_e2m1fn_x4
ALU = mybir.AluOpType
ACT = mybir.ActivationFunctionType

P = 128
PASSES = 2
TILES = H // P
BANK = 512
FIRST = 256
FUSED = 2


def tile_list_frost_page_rewrite_kernel(
    tc, tab_words, tab_scales, offs, w1, b1, base, wgs, page0, offs2, offs3, d,
    w2_words, w2_scales, b2, wgo, offs4, out,
):
    nc = tc.nc
    with ExitStack() as ctx:
        lists = ctx.enter_context(tc.tile_pool(name="lists", bufs=1))
        keep = ctx.enter_context(tc.tile_pool(name="keep", bufs=1))
        ring = ctx.enter_context(tc.tile_pool(name="ring", bufs=2))
        acc_pool = ctx.enter_context(tc.psum_pool(name="acc", bufs=4))
        turn_pool = ctx.enter_context(tc.psum_pool(name="turn", bufs=2))

        def load_list(name, src):
            tile = lists.tile([P, S // 16], U16, name=name)
            nc.sync.dma_start(tile[:], src)
            return tile

        def cols16(tile, lo, hi):
            return tile[:, lo // 16 : hi // 16]

        idx = load_list("idx", offs)
        tab_sc = keep.tile([P, T], U8, name="tab_sc", align_bytes=64)
        nc.vector.memset(tab_sc[:].bitcast(I32), 0)
        for q in range(4):
            nc.sync.dma_start(
                tab_sc[32 * q : 32 * q + 8, :].bitcast(I32),
                tab_scales[:, 4 * q : 4 * q + 4, :].bitcast(I32),
            )

        def load_table(a):
            tile = keep.tile([P, T], I32, name="tab%d" % a, tag="big%d" % a, align_bytes=64)
            nc.sync.dma_start(tile[:], tab_words[a].rearrange("p t i -> p (t i)").bitcast(I32))
            return tile

        tab0 = load_table(0)

        ident32 = keep.tile([P, P], F32, name="ident32")
        ident16 = keep.tile([P, P], BF16, name="ident16")

        def load_vectors(name, vectors):
            rows = keep.tile([P, P], F32, name=name + "_rows")
            nc.gpsimd.memset(rows[:], 0.0)
            for n, vec in enumerate(vectors):
                nc.sync.dma_start(rows[TILES * n : TILES * (n + 1), :], vec.rearrange("(i p) -> i p", p=P))
            bank = turn_pool.tile([P, P], F32, name=name + "_bank", tag="second")
            nc.tensor.transpose(bank[:], rows[:], ident32[:])
            cols = keep.tile([P, len(vectors) * TILES], F32, name=name + "_cols")
            nc.scalar.copy(cols[:], bank[:, 0 : len(vectors) * TILES])
            return cols

        make_identity(nc, ident32[:])
        make_identity(nc, ident16[:])

        v_sc = keep.tile([P, S], U8, name="v_sc", align_bytes=64)
        nc.vector.tensor_copy(v_sc[:], tab_sc[:].indirect(idx[:]))
        v_codes = [keep.tile([P, S], U32, name="v_codes%d" % a, align_bytes=64) for a in range(PASSES)]
        nc.vector.tensor_copy(v_codes[0][:], tab0[:].bitcast(U32).indirect(idx[:]))

        w1_mx = {}
        held = {}

        def weave_w1(first, last):
            n = last - first
            woven = keep.tile([P, n, PASSES, P // 4, 4, 4], BF16, name="w1_woven%d" % first,
                              tag="woven%d" % first, align_bytes=64)
            for a in range(PASSES):
                raw = keep.tile([P, 4, n * P], F32, name="w1_raw%d_%d" % (first, a),
                                tag="raw%d_%d" % (first, a), align_bytes=64)
                nc.sync.dma_start(
                    raw[:],
                    w1[512 * a : 512 * (a + 1), first * P : last * P].rearrange("(p j) c -> p j c", j=4),
                )
                nc.scalar.copy(
                    woven[:, :, a].rearrange("p n c i j -> p n c j i"),
                    raw[:].rearrange("p j (n c i) -> p n c j i", n=n, i=4),
                )
            held["woven", first] = woven

        def quantise_w1(first, last, tag):
            n = last - first
            woven = held["woven", first]
            codes = keep.tile([P, n * PASSES * P], U32, name="w1_codes%d" % first, align_bytes=64)
            scales = keep.tile([P, n * PASSES * P], U8, name="w1_scales%d" % first, tag=tag, align_bytes=64)
            nc.vector.quantize_mx(
                codes[:].bitcast(E4M3), scales[:], woven[:].rearrange("p n a c i j -> p (n a c i j)")
            )
            for i in range(first, last):
                for a in range(PASSES):
                    lo = ((i - first) * PASSES + a) * P
                    w1_mx[i, a] = (codes[:, lo : lo + P].bitcast(E4M3), scales[:, lo : lo + P])

        pages = []
        picked = {}
        z_codes = {1: keep.tile([P, E], U32, name="z_codes1", align_bytes=64)}
        feats = {}
        z_sc = [keep.tile([P, E], U8, name="z_sc%d" % a, align_bytes=64) for a in range(PASSES)]

        def load_base(i):
            base_i = ring.tile([P, S], F32, name="base_i", bufs=3)
            nc.sync.dma_start(base_i[:], base[i * P : (i + 1) * P, :])
            return base_i

        def features(i, base_i, h, first, end):
            feats[i, first] = h
            for lo in range(first, end, BANK):
                acc = acc_pool.tile([P, BANK], F32, name="acc")
                for a in range(PASSES):
                    nc.tensor.matmul_mx(
                        acc[:], lhsT=w1_mx[i, a][0], lhsT_scale=w1_mx[i, a][1],
                        rhs=v_codes[a][:, lo : lo + BANK].bitcast(E4M3),
                        rhs_scale=v_sc[4 * a :, lo : lo + BANK],
                        start=(a == 0), stop=(a == PASSES - 1),
                    )
                nc.vector.scalar_tensor_tensor(
                    h[:, lo - first : lo - first + BANK], acc[:], held["b1"][:, i : i + 1], base_i[:, lo : lo + BANK],
                    ALU.add, ALU.max,
                )
            if i >= FUSED:
                nc.gpsimd.tensor_tensor(h[:], h[:], held["wgs"][:], ALU.mult)

        def load_page(i):
            page = keep.tile([P, T2], F32, name="page%d" % i)
            nc.sync.dma_start(page[:], page0[i * P : (i + 1) * P, :])
            pages.append(page)

        def place(i, lo, hi):
            window = pages[i][:].indirect(cols16(held["idx2"], lo, hi))
            if i >= FUSED:
                nc.vector.tensor_copy(window, feats[i, lo][:])
            else:
                nc.vector.tensor_tensor(window, feats[i, lo][:], held["wgs"][:, lo:hi], ALU.mult)

        def pick(i, lo, hi, x, th):
            nc.vector.tensor_copy(x, pages[i][:].indirect(cols16(held["idx3"], lo, hi)))
            nc.scalar.activation(th, x, ACT.Tanh, scale=held["vecs"][:, i : i + 1])
            picked[i, lo, hi] = (x, th)

        z_turned = {(0, 0): keep.tile([P, E // P, 2, P], F32, name="zt0", align_bytes=64)}

        def turn(i, lo, hi, z, engine):
            x, th = picked[i, lo, hi]
            engine.tensor_tensor(z, x, th, ALU.mult)
            groups = (hi - lo) // P
            bank = turn_pool.tile([P, groups, P], BF16, name="first")
            for g in range(groups):
                nc.tensor.transpose(bank[:, g, :], z[:, g * P : (g + 1) * P], ident16[:])
            words = bank[:].bitcast(F32).rearrange("p g (m e) -> p g e m", e=2)
            a, u = divmod(i, 4)
            cuts = [lo, hi] if (a == 0 or lo > 0 or hi == FIRST) else [lo, FIRST, hi]
            for c0, c1 in zip(cuts, cuts[1:]):
                nc.scalar.copy(
                    z_turned[a, c0][:, :, :, 32 * u : 32 * (u + 1)],
                    words[:, (c0 - lo) // P : (c1 - lo) // P],
                )

        def quantise_z(a, lo, hi, tag, held_from):
            woven = keep.tile([P, (hi - lo) * 4], BF16, name="z_woven%d_%d" % (a, lo), tag=tag, align_bytes=64)
            words = woven[:].bitcast(F32)
            for g0 in range(0, (hi - lo) // P, 2):
                bank = turn_pool.tile([P, 2, 2, P], F32, name="second", tag="second")
                for g in range(2):
                    for e in range(2):
                        nc.tensor.transpose(bank[:, g, e, :], z_turned[a, held_from][:, (lo - held_from) // P + g0 + g, e, :], ident32[:])
                nc.scalar.copy(
                    words[:, g0 * 2 * P : (g0 + 2) * 2 * P].rearrange("p (g j e) -> p g j e", g=2, e=2),
                    bank[:].rearrange("p g e j -> p g j e"),
                )
            nc.vector.quantize_mx(z_codes[a][:, lo:hi].bitcast(E4M3), z_sc[a][:, lo:hi], woven[:])

        last = TILES - 1
        weave_w1(0, 1)
        quantise_w1(0, 1, "scales0")
        tab1 = load_table(1)
        for lo in range(0, S, BANK):
            nc.vector.tensor_copy(
                v_codes[1][:, lo : lo + BANK], tab1[:].bitcast(U32).indirect(cols16(idx, lo, lo + BANK))
            )
        held["b1"] = load_vectors("b1", [b1])
        base0 = load_base(0)
        features(0, base0, keep.tile([P, BANK], F32, name="h0a", tag="h0", align_bytes=64), 0, BANK)
        held["wgs"] = keep.tile([P, S], F32, name="wgs_sb")
        nc.sync.dma_start(held["wgs"][:], wgs)
        held["idx2"] = load_list("idx2", offs2)
        load_page(0)
        place(0, 0, BANK)
        weave_w1(1, 2)
        quantise_w1(1, 2, "scales1")
        features(0, base0, keep.tile([P, BANK], F32, name="h0b", tag="woven1", align_bytes=64), BANK, S)
        place(0, BANK, S)
        features(1, load_base(1), keep.tile([P, S], F32, name="h1", tag="raw0_0", align_bytes=64), 0, S)
        weave_w1(2, 4)
        quantise_w1(2, 4, "scales2")
        held["idx3"] = load_list("idx3", offs3)
        held["vecs"] = load_vectors("d_b2", [d, b2])
        x0 = keep.tile([P, E], F32, name="x0", tag="woven2", align_bytes=64)
        features(2, load_base(2), keep.tile([P, S], F32, name="h2", tag="h0", align_bytes=64), 0, S)
        weave_w1(4, 8)
        load_page(1)
        pick(0, 0, E, x0[:], keep.tile([P, E], F32, name="th0", tag="raw4_1", align_bytes=64)[:])
        for i in range(1, TILES):
            if i > 1:
                load_page(i)
            place(i, 0, S)
            if i == 1:
                quantise_w1(4, 8, "raw0_0")
            if i == 4:
                z_turned[1, 0] = keep.tile([P, FIRST // P, 2, P], F32, name="zt1a", tag="raw2_0", align_bytes=64)
                z_turned[1, FIRST] = keep.tile(
                    [P, (E - FIRST) // P, 2, P], F32, name="zt1b", tag="raw4_1", align_bytes=64
                )
            if i == last:
                pick(i, 0, FIRST, keep.tile([P, FIRST], F32, name="x_last_a", tag="x_last")[:],
                     ring.tile([P, FIRST], F32, name="th")[:])
                z = keep.tile([P, FIRST], BF16, name="z%d" % (i - 1), tag="h%d" % (i % 2), align_bytes=64)
                turn(i - 1, 0, FIRST, z[:], nc.vector)
            else:
                if i == 1:
                    z = keep.tile([P, E], BF16, name="z0", tag="woven4", align_bytes=64)
                    turn(0, 0, E, z[:], nc.gpsimd)
                hi = FIRST if i == last - 1 else E
                if i == 4:
                    x = keep.tile([P, hi], F32, name="x4", tag="zc0", align_bytes=64)
                else:
                    x = ring.tile([P, hi], F32, name="x", align_bytes=64)
                pick(i, 0, hi, x[:], ring.tile([P, hi], F32, name="th")[:])
                if i + 2 < TILES:
                    h = keep.tile([P, S], F32, name="h%d" % (i + 2), tag="h%d" % (i % 2), align_bytes=64)
                    features(i + 2, load_base(i + 2), h, 0, S)
                if i < last - 1:
                    z = ring.tile([P, E], BF16, name="z", align_bytes=64)
                    turn(i, 0, E, z[:], nc.gpsimd)
                if i == 4:
                    z_codes[0] = keep.tile([P, E], U32, name="z_codes0", tag="zc0", align_bytes=64)
                    quantise_z(0, 0, E, "big0", 0)

        w2 = keep.tile([P, PASSES, 2 * H], U8, name="w2", tag="woven4", align_bytes=64)
        nc.sync.dma_start(w2[:].bitcast(I32), w2_words.rearrange("a p n -> p a n").bitcast(I32))
        w2_sc = keep.tile([P, PASSES, H], U8, name="w2_sc", align_bytes=64)
        nc.gpsimd.memset(w2_sc[:].bitcast(I32), 0)
        for q in range(4):
            nc.sync.dma_start(
                w2_sc[32 * q : 32 * q + 4].bitcast(I32),
                w2_scales[:, 4 * q : 4 * q + 4, :].rearrange("a r n -> r a n").bitcast(I32),
            )
        wgo_sb = keep.tile([P, E], F32, name="wgo_sb", tag="woven2", align_bytes=64)
        nc.sync.dma_start(wgo_sb[:], wgo)
        idx4 = load_list("idx4", offs4)

        z_last_a = keep.tile([P, FIRST], BF16, name="z_last_a", align_bytes=64)
        turn(last, 0, FIRST, z_last_a[:], nc.vector)
        quantise_z(1, 0, FIRST, "woven_a", 0)
        x_rest = keep.tile([P, 2, E - FIRST], F32, name="x_rest", tag="x_last")
        th_rest = keep.tile([P, 2, E - FIRST], F32, name="th_rest", tag="raw2_0", align_bytes=64)
        pick(last - 1, FIRST, E, x_rest[:, 0, :], th_rest[:, 0, :])
        pick(last, FIRST, E, x_rest[:, 1, :], th_rest[:, 1, :])
        z_rest = keep.tile([P, 2, E - FIRST], BF16, name="z_rest", tag="woven_a", align_bytes=64)
        turn(last - 1, FIRST, E, z_rest[:, 0, :], nc.vector)
        turn(last, FIRST, E, z_rest[:, 1, :], nc.vector)

        def second_stage(n, lo, hi, cuts, tag, bufs):
            y = (keep if bufs == 1 else ring).tile([P, hi - lo], F32, name="y", tag=tag, bufs=bufs, align_bytes=64)
            for c0, c1 in zip(cuts, cuts[1:]):
                acc = acc_pool.tile([P, c1 - c0], F32, name="acc")
                for a in range(PASSES):
                    nc.tensor.matmul_mx(
                        acc[:], lhsT=w2[:, a, 2 * P * n : 2 * P * (n + 1)].bitcast(E2M1),
                        lhsT_scale=w2_sc[:, a, P * n : P * (n + 1)],
                        rhs=z_codes[a][:, c0:c1].bitcast(E4M3), rhs_scale=z_sc[a][:, c0:c1],
                        start=(a == 0), stop=(a == PASSES - 1),
                    )
                mag = ring.tile([P, c1 - c0], F32, name="mag")
                nc.scalar.activation(mag[:], acc[:], ACT.Abs)
                nc.scalar.activation(
                    y[:, c0 - lo : c1 - lo], mag[:], ACT.Identity, bias=held["vecs"][:, TILES + n : TILES + n + 1]
                )
            nc.vector.tensor_tensor(pages[n][:].indirect(cols16(idx4, lo, hi)), y[:], wgo_sb[:, lo:hi], ALU.mult)

        early = 6
        second_stage(0, 0, FIRST, [0, FIRST], "y_first", 3)
        quantise_z(1, FIRST, BANK, "h0", FIRST)
        quantise_z(1, BANK, E, "big1", FIRST)
        for n in range(1, early):
            tag = {early - 2: "h0", early - 1: "big1"}.get(n, "y_first")
            second_stage(n, 0, FIRST, [0, FIRST], tag, 3 if tag == "y_first" else 1)
        for n in range(TILES):
            if n < early:
                second_stage(n, FIRST, E, [FIRST, BANK, E], "x", 2)
            else:
                second_stage(n, 0, E, [0, BANK, E], "x", 2)
            nc.sync.dma_start(out[n * P : (n + 1) * P, :], pages[n][:])
